import numpy as np, ml_dtypes
CORES = [66,74,82,90,194,202,210,218]
N = 8
import mx_ref
BF = ml_dtypes.bfloat16
def entries(a):
    return np.ascontiguousarray(a.T).reshape(-1)
def table(e):
    return np.ascontiguousarray(np.reshape(e, (-1, 16)).T).astype(np.int32)
def pick(q, e):
    c = np.concatenate([q[0].reshape(128, -1, 4), np.zeros((128, 1, 4), np.uint8)], axis=1); s = np.concatenate([q[1], np.ones((16, 1), np.uint8)], axis=1)
    return (np.ascontiguousarray(c[:, e].reshape(128, -1)), np.ascontiguousarray(s[:, e]))
def join(*qs):
    return (np.concatenate([q[0] for q in qs], axis=1), np.concatenate([q[1] for q in qs], axis=1))
def put(q, e, v):
    c, s = q[0].reshape(128, -1, 4).copy(), q[1].copy(); c[:, e] = v[0].reshape(128, -1, 4); s[:, e] = v[1]
    return (c.reshape(128, -1), s)
def pk(c, s):
    return (np.ascontiguousarray(c), mx_ref.live(s))
def emit(q):
    return q[0], q[1]
def packed(v, rng):
    q = [mx_ref.quantize(np.ascontiguousarray(v[r])) for r in range(N)]
    return np.stack([a for a, b in q]), np.stack([mx_ref.plane(b, rng) for a, b in q])
def f(rng, *shape):
    return mx_ref.flush((rng.standard_normal(shape, dtype=np.float32) * np.exp2(rng.integers(-2, 3, shape[:-1] + (1,)))).astype(BF))
def wide(rng, *shape, cols=0):
    v = rng.standard_normal(shape, dtype=np.float32) * np.exp2(rng.integers(-12, 13, shape)).astype(np.float32)
    if cols: v *= np.repeat(np.exp2(rng.integers(-cols, cols + 1, shape[:-2] + (1, shape[-1] // 4))) * (rng.random(shape[:-2] + (1, shape[-1] // 4)) > 0.0625), 4, axis=-1).astype(np.float32)
    return mx_ref.flush(v.astype(BF))
C, CB, CAPP, S = 256, 80, 48, 288
def counts(rng, total, cap, least):
    n = np.array(least)
    while n.sum() < total: n[rng.choice(np.flatnonzero(n < cap))] += 1
    return n
def runs(rng, least, cap):
    n = np.zeros((N, N), int)
    for s in range(N)[::-1]: n[s] = counts(rng, C, np.minimum(cap[s], CAPP + n[N - 1]), least[s])
    return n
def keeps(rng, n, fall=0, least=np.zeros((N, N), int)):
    k = np.zeros((N, N), int)
    for s in range(N)[::-1]:
        above = k.sum(axis=0)
        k[s] = np.clip(np.minimum(rng.integers(0, 2 * n[s] // 3 + 1), n[s] - fall), np.maximum(n[s] - above, least[s]), np.minimum(np.minimum(n[s], CAPP), S - above))
    return k
def lists(rng, n, k, ends=False, narrow=False):
    p = np.sort(rng.choice(65536 - 2 * N * S, N - 1, replace=False)) + 2 * S * np.arange(1, N)
    if ends: p[0] = int(k[:, 0].sum()) + 2 + int(rng.integers(0, 4))
    if narrow: p[-1] = 65535
    lo, hi = np.append(0, p), np.append(p, 65536)
    keys = [[] for s in range(N)]
    for d in range(N):
        e, i, j = int(ends), -1, -1
        u = lo[d] + e + rng.choice(int(hi[d] - lo[d]) - 2 * e, int(k[:, d].sum()), replace=False)
        at = np.append(np.cumsum(k[::-1, d])[::-1], 0)[1:]
        if ends:
            low, c = np.flatnonzero(n[:, d] - k[:, d] > 1), np.flatnonzero(k[:, d] > 1)
            c = c[c > low[0]]
            if d in (0, N - 1): c = c[c < N - 1]
            i = rng.choice(c); j = rng.choice(low[low < i])
            u[at[i]] = lo[d]; u[at[i] + 1] = hi[d] - 1
        for s in range(N):
            m = at[i] + np.arange(2) if s == j else np.zeros(0, int)
            old = np.concatenate([m, rng.permutation(np.setdiff1d(np.arange(at[s]), m))])[:n[s, d] - k[s, d]]
            keys[s].append(u[np.concatenate([old, at[s] + np.arange(k[s, d])])])
    return {"ky": np.stack([table(np.sort(np.concatenate(v))) for v in keys]), "sp": np.stack([table(np.append(p, np.full(17 - N, 65535)))] * N)}
def setup_inputs(rng):
    kc, ks = packed(f(rng, N, 128, 4 * C), rng)
    n = runs(rng, rng.integers(1, CAPP // 2 + 1, (N, N)), np.full((N, N), CB))
    return {"kc": kc, "ks": ks, "w": f(rng, N, 128, 512), **lists(rng, n, keeps(rng, n))}
def setup_inputs_single(rng):
    least, cap = rng.integers(1, CAPP // 2 + 1, (N, N)), np.full((N, N), CB)
    least[:, N - 1] = rng.integers(0, 2, N); least[rng.permutation(N - 1)[:2], N - 1] = 1; cap[:, N - 1] = least[:, N - 1]
    n = runs(rng, least, cap)
    return {**setup_inputs(rng), **lists(rng, n, keeps(rng, n), narrow=True)}
def setup_inputs_narrow(rng):
    least, cap = rng.integers(1, CAPP // 2 + 1, (N, N)), np.full((N, N), CB)
    least[:, N - 1] = 0; cap[:, N - 1] = 0
    n = runs(rng, least, cap)
    return {**setup_inputs(rng), **lists(rng, n, keeps(rng, n), narrow=True)}
def setup_inputs_full(rng):
    h = int(rng.integers(0, N)); least = np.ones((N, N), int)
    a = np.append(h, rng.permutation(np.delete(np.arange(N), h)))[:(C - N) // CAPP]
    least[N - 1, a] = CAPP
    for s in range(N - 1): least[s, np.append(h, rng.permutation(a[1:]))[:(C - N) // CB]] = CB
    n = runs(rng, least, np.full((N, N), CB)); k = keeps(rng, n)
    v = np.zeros(N, int); v[N - 2:] = CAPP; v[rng.permutation(N - 2)[:S // CAPP - 2]] = CAPP
    k[:, h] = counts(rng, S, CAPP, v)
    return {**setup_inputs(rng), **lists(rng, n, k)}
def setup_inputs_edges(rng):
    q = int(rng.integers(1, N)); h = int(rng.choice(np.delete(np.arange(N - 1), min(q, N - 2))))
    least, cap = rng.integers(2, CAPP // 2 + 1, (N, N)), np.full((N, N), CB)
    least[h, q] = 0; cap[h, q] = 0
    few = rng.integers(2, 5, N)
    few[rng.permutation(np.setdiff1d(np.arange(N), [int(rng.integers(0, N - 2)), N - 2]))[:int(rng.integers(2, N - 1))]] = 0
    least[:, 0] = few; cap[:, 0] = few
    n = runs(rng, least, cap)
    two = np.zeros((N, N), int); two[N - 2, [0, N - 1]] = 2
    return {**setup_inputs(rng), **lists(rng, n, keeps(rng, n, 2, two), ends=True)}
def setup_inputs_spread(rng):
    d = setup_inputs(rng); d["kc"], d["ks"] = packed(wide(rng, N, 128, 4 * C, cols=8), rng); return d
def check_inputs(d):
    b = []
    p = entries(d["sp"][0]).astype(np.int64); g = p[:N - 1]
    if (d["sp"] != d["sp"][:1]).any() or (p[N - 1:] != 65535).any() or g.min() < 1 or g.max() > 65535 or (np.diff(g) <= 0).any(): b.append("sp")
    lo, hi = np.append(0, g), np.append(g, 65536)
    k = [entries(d["ky"][s]).astype(np.int64) for s in range(N)]
    bad = any(v.min() < 0 or v.max() > 65535 or (np.diff(v) <= 0).any() for v in k)
    x, s = np.concatenate(k), np.repeat(np.arange(N), C)
    o = np.argsort(x, kind="stable"); o = o[np.append(x[o][1:] != x[o][:-1], True)]
    x, s = x[o], s[o]
    for q in range(N):
        m = (x >= lo[q]) & (x < hi[q])
        if max(((v >= lo[q]) & (v < hi[q])).sum() for v in k) > CB or m.sum() > S or np.bincount(s[m], minlength=N).max() > CAPP: bad = True
    if bad: b.append("ky")
    return b
def reference(kc, ks, w, ky, sp):
    every = join(*[pk(kc[s], ks[s]) for s in range(N)])
    keys = np.concatenate([entries(ky[s]) for s in range(N)])
    oc, osc = np.zeros((N, 128, 4 * S), np.uint8), np.zeros((N, 16, S), np.uint8)
    ok, y = np.zeros((N, 2, S), np.float32), np.zeros((N, 128, S), np.float32)
    for d in range(N):
        p = entries(sp[d])[:N - 1]
        lo, hi = np.append(0, p)[d], np.append(p, 65536)[d]
        e = np.flatnonzero((keys >= lo) & (keys < hi))
        e = e[np.argsort(keys[e], kind="stable")]
        e = e[np.append(keys[e][1:] != keys[e][:-1], True)[:e.size]]
        a = np.full(S, -1); a[:e.size] = e
        kept = pick(every, a)
        oc[d], osc[d] = emit(kept)
        ok[d, 0] = np.where(a >= 0, keys[a], -1); ok[d, 1] = np.where(a >= 0, a // C, -1)
        y[d] = mx_ref.matmul(mx_ref.quantize(np.ascontiguousarray(w[d])), kept)
    return {"oc": oc, "osc": osc, "ok": ok, "y": y}

from concourse.bass import DstId, RemoteDMATransfer
from concourse.mybir import dt, AluOpType as A, AxisListType, ActivationFunctionType as AF

N, C, CAPP, S = 8, 256, 48, 288
SLOTS = N * CAPP
ZC = SLOTS // 2
ZE = ZC + 16
FIN = SLOTS + 16


def at(s):
    return CAPP * s + (16 if CAPP * s >= ZC else 0)


F32, BF, I32, U16, CODE, U8 = "float32", "bfloat16", "int32", "uint16", "float8_e4m3fn_x4", "uint8"
SCRATCH = {
    "land": ("dram", [N, 128, 2], I32),
    "land3": ("dram", [N, 128, 6], U16),
    "f1": ("sbuf", [64, 16], F32), "f2": ("sbuf", [32, 16], F32),
    "g1": ("sbuf", [64, 36], F32), "g2": ("sbuf", [32, 36], F32), "g3": ("sbuf", [32, 18], F32),
    "acc": ("psum", [128, 1024], F32),
}
for _d, _l in ((I32, "lk 16, owni 16, spi 16, spb 16, pidx 1, q16 1, blk 1, half 1, il8 16, il16 32, idg 32, hi 3"),
               (U16, "lku 16, ownu 16, e8 16, eh 16, e16 32, edg 32, wl 24, m6 6, ix 8, ou 6, ol 18"),
               (BF, "win 65536, ones 256, vals 256, vals2 96, hb 256, xt 256, f3 8, ex 256, lin 256, junk 1024, cmp 514, zt 512, "
                    "wt 512, junk2 800, cmp2 402, L 2400, LT 576"),
               (F32, "lkf 16, ownf 16, spf 16, q16f 1, halff 1, b96 1, c1 1, c2 1, c3 1, c4 1, c5 1, it6 6, bt 6, tt6 6, itr 3, "
                     "trash 3, iv 96, rk 400, tmp 128, tmpb 64, tmpc 32, basew 16, baseb 256, base 256, num 256, cnt 6, wf 24, "
                     "kx 512, kg 512, kl 544, k96 96, kt 96, kf 400, inv 3, tr 3, s2 3, pos 3, h16 3, h32 3, okk 288, okr 288, "
                     "yfin 400, ysb 288"),
               (CODE, "kown 272, slot 384, fin 400, ord 288, wq 128, zq 128"),
               (U8, "kowns 272, slots 384, fins 400, ords 288, wqs 128, zqs 128")):
    for _e in _l.split(", "):
        SCRATCH[_e.split(" ")[0]] = ("sbuf", [128, int(_e.split(" ")[1])], _d)
SEMAPHORES = ["v", "s", "gc1", "gc2", "gc3", "mm", "lland", "lown", "lsp", "lk", "lw", "larr", "lmsg", "lix", "lfin", "lzero",
              "st", "akey", "acode", "ascale", "amsg", "xkey", "xcode", "xscale", "xmsg"]


def rank_program(g, core, T, topo):
    r = T.rank_of(core)
    if r is None:
        return
    M = T.sem
    others = [d for d in range(N) if d != r]
    n = {"v": 0, "s": 0}

    def V(call, *a, dep=True):
        if dep and n["v"]:
            g.vector.wait_ge(M.v, n["v"])
        call(*a).then_inc(M.v, 1)
        n["v"] += 1

    def act(*a, dep=True, **k):
        if dep and n["s"]:
            g.scalar.wait_ge(M.s, n["s"])
        g.scalar.activation(*a, **k).then_inc(M.s, 1)
        n["s"] += 1

    tc, tt, ts = g.vector.tensor_copy, g.vector.tensor_tensor, g.vector.tensor_scalar
    ms, tp, red = g.vector.memset, g.vector.transpose, g.vector.tensor_reduce

    def dst(d):
        rid, pid = topo.addr(T.cores[d], core)
        return DstId(rid=rid, pnc=pid)

    def eng(d, k):
        return 1 << topo.engines(core, T.cores[d])[k]

    def iota(sem, out, pattern, base, f=True):
        if f:
            g.iota(out, pattern, base, 0, allow_small_or_imprecise_dtypes=True).then_inc(sem, 1)
        else:
            g.iota(out, pattern, base, 0).then_inc(sem, 1)

    g.sync.dma_start(T.land[r], T.ky[:]).then_inc(M.lland, 16)
    for h in range(2):
        g.scalar.dma_start(T.owni[16 * h:16 * h + 16, :], T.ky[:]).then_inc(M.lown, 16)
    g.sync.dma_start(T.spi[0:1, :], T.sp[:]).then_inc(M.lsp, 16)
    for a, b in ((0, C), (C, 272)):
        g.scalar.dma_start(T.kown[:, a:b].bitcast(dt.uint8), T.kc[:, 0:4 * (b - a)]).then_inc(M.lk, 16)
        g.scalar.dma_start(T.kowns[:, a:b], T.ks[:, 0:b - a]).then_inc(M.lk, 16)
    g.scalar.dma_start(T.wt[:], T.w[:]).then_inc(M.lw, 16)

    g.iota(T.pidx[:], [[0, 1]], 0, 1).then_inc(M.gc1, 1)
    iota(M.gc1, T.il8[:], [[1, 8], [0, 2]], 0, False)
    iota(M.gc1, T.it6[:], [[16, 6]], 0)
    g.wait_ge(M.lland, 16)
    g.remote_dma_fused([RemoteDMATransfer(dst_ids=[dst(d)], dma_engine_mask=eng(d, k), remote_sem=M.akey,
                                          src=T.land[r], dst=T.land[r]) for k, d in enumerate(others)], local_sem=M.xkey)
    V(ms, T.ones[:], 1.0)
    g.wait_ge(M.lsp, 16)
    g.partition_broadcast(T.spb[:], T.spi[0:1, :], 128).then_inc(M.gc2, 1)
    g.wait_ge(M.v, n["v"])
    g.affine_select(T.vals[:], T.ones[:], [[0, 256]], A.is_ge, 0.0, 16 * (r + 1) - 1, -1).then_inc(M.gc2, 1)
    iota(M.gc3, T.iv[:], [[0, 2], [32, 3], [1, 16]], 0)
    iota(M.gc3, T.il16[:], [[1, 16], [0, 2]], 0, False)
    iota(M.gc3, T.idg[:], [[16, 2], [32, 16]], 0, False)
    iota(M.gc3, T.itr[:], [[512, 3]], 832)
    iota(M.gc3, T.rk[:, 0:ZC], [[1, 4], [0, CAPP]], 0)
    iota(M.gc3, T.rk[:, ZE:FIN], [[1, 4], [0, CAPP]], 4)

    g.vector.wait_ge(M.gc1, 3)
    V(ts, T.q16[:], T.pidx[:], 15, None, A.bitwise_and)
    V(ts, T.blk[:], T.pidx[:], 5, None, A.logical_shift_right, dep=False)
    V(ts, T.half[:], T.pidx[:], 4, 1, A.logical_shift_right, A.bitwise_and, dep=False)
    V(tc, T.e8[:], T.il8[:], dep=False)
    V(ms, T.tmp[:, 112:128], 0.0, dep=False)
    V(ms, T.cmp[:, 256:257], -256.0, dep=False)
    V(ms, T.cmp[:, 513:514], -256.0, dep=False)
    g.vector.wait_ge(M.lown, 32)
    for a in range(4):
        V(tc, T.ownf[32 * a:32 * a + 32, :], T.owni[0:32, :], dep=not a)
    V(tc, T.q16f[:], T.q16[:], dep=False)
    V(tc, T.halff[:], T.half[:], dep=False)
    V(ts, T.b96[:], T.blk[:], 96.0, None, A.mult, dep=False)
    V(tc, T.ownu[:], T.ownf[:])
    V(ts, T.eh[:], T.il8[:], 2.0, T.halff[:], A.mult, A.add, dep=False)
    V(tt, T.c2[:], T.b96[:], T.q16f[:], A.add, dep=False)
    V(tc, T.win[:].indirect(T.ownu[:]), T.ones[:])
    V(ts, T.tt6[:], T.it6[:], T.c2[:], 0.5, A.add, A.add, dep=False)
    g.vector.wait_ge(M.gc2, 2)
    V(tc, T.spf[:], T.spb[:])
    V(ts, T.bt[:], T.tt6[:], -1.0, None, A.mult, dep=False)
    for j in range(N - 1):
        V(ts, T.tmp[:, 16 * j:16 * j + 16], T.ownf[:], T.spf[:, j:j + 1], float(CAPP), A.is_ge, A.mult, dep=not j)
    V(tt, T.tmpb[:], T.tmp[:, 0:64], T.tmp[:, 64:128], A.add)
    V(tt, T.tmpc[:], T.tmpb[:, 0:32], T.tmpb[:, 32:64], A.add)
    V(tt, T.basew[:], T.tmpc[:, 0:16], T.tmpc[:, 16:32], A.add)
    V(tc, T.baseb[:], T.basew[:].indirect(T.eh[:]))
    V(tp, T.base[:], T.baseb[:])

    g.sync.wait_ge(M.lland, 16)
    g.sync.wait_ge(M.akey, N - 1)
    g.sync.dma_start(T.lk[:], T.land[:]).then_inc(M.larr, 16)
    g.vector.wait_ge(M.larr, 16)
    V(tc, T.lku[:], T.lk[:])
    V(tc, T.win[:].indirect(T.lku[:]), T.vals[:])
    V(tc, T.hb[:], T.win[:].indirect(T.ownu[:]))
    V(tp, T.xt[:], T.hb[:])
    V(tt, T.f1[:], T.xt[0:64, 0:256:16], T.xt[64:128, 0:256:16], A.min)
    V(tt, T.f2[:], T.f1[0:32, :], T.f1[32:64, :], A.min)
    for a in range(4):
        V(tt, T.f3[32 * a:32 * a + 32, :], T.f2[:, 0:16:2], T.f2[:, 1:16:2], A.min, dep=not a)
    V(tc, T.ex[:], T.f3[:].indirect(T.e8[:]))
    V(tp, T.lin[:], T.ex[:])
    V(g.vector.tensor_tensor_scan, T.num[:], T.base[:], T.lin[:], 0.0, A.max, A.add)
    nnum = n["v"]
    g.scalar.wait_ge(M.v, nnum)
    for k in range(4):
        act(T.junk[:, 256 * k:256 * k + 256], T.num[:], AF.Sign, dep=False, bias=T.bt[:, k:k + 1], scale=1.0, accum_out=T.cnt[:, k:k + 1])
    for k in range(2):
        V(ts, T.cmp[:, 257 * k:257 * k + 256], T.num[:], T.tt6[:, 4 + k:5 + k], 2.0, A.is_gt, A.mult, dep=not k)
    for k in range(2):
        V(red, T.cnt[:, 4 + k:5 + k], T.cmp[:, 257 * k:257 * k + 257], AxisListType.X, A.add, dep=not k)
    ncnt = n["v"]
    g.vector.wait_ge(M.s, n["s"])
    V(ts, T.m6[:], T.cnt[:], -0.5, 128.0, A.mult, A.add)
    nm6 = n["v"]
    g.scalar.wait_ge(M.v, ncnt)
    for x in range(4):
        o = x + 1 - 2 * (x % 2)
        act(T.wf[32 * x:32 * x + 32, 6 * o:6 * o + 6], T.cnt[32 * o:32 * o + 32, :], AF.Copy, dep=not x)
    for x in range(4):
        V(tc, T.wf[32 * x:32 * x + 32, 6 * x:6 * x + 6], T.cnt[32 * x:32 * x + 32, :], dep=not x)
    g.vector.wait_ge(M.s, n["s"])
    for i in range(4):
        f, to = i // 2, i % 2
        V(ts, T.wl[64 * to:64 * to + 64, 12 * f:12 * f + 12], T.wf[64 * f:64 * f + 64, 12 * f:12 * f + 12], -0.5, 128.0, A.mult, A.add, dep=not i)
    nwl = n["v"]
    g.vector.wait_ge(M.lk, 64)
    V(tc, T.slot[:].bitcast(dt.uint32), T.kown[:].bitcast(dt.uint32).indirect(T.wl[:]))
    nslot = n["v"]
    g.scalar.wait_ge(M.lk, 64)
    g.scalar.wait_ge(M.v, nwl)
    act(T.slots[:], T.kowns[:].indirect(T.wl[:]), AF.Copy)
    nslots = n["s"]
    for a, b, sa, sx, nm, bc in ((T.slot, T.fin, M.acode, M.xcode, nslot, True), (T.slots, T.fins, M.ascale, M.xscale, nslots, False)):
        g.wait_ge(M.v if bc else M.s, nm)
        tr = []
        for k, d in enumerate(others):
            x, z = a[:, CAPP * d:CAPP * d + CAPP], b[:, at(r):at(r) + CAPP]
            if bc:
                x, z = x.bitcast(dt.uint8), z.bitcast(dt.uint8)
            tr.append(RemoteDMATransfer(dst_ids=[dst(d)], dma_engine_mask=eng(d, k), remote_sem=sa, src=x, dst=z))
        g.remote_dma_fused(tr, local_sem=sx)
    g.sync.wait_ge(M.v, nm6)
    for a in range(4):
        g.sync.dma_start(T.land3[r, a:128:4, :], T.m6[32 * a:32 * a + 32, :]).then_inc(M.lmsg, 16)
    g.wait_ge(M.lmsg, 64)
    g.remote_dma_fused([RemoteDMATransfer(dst_ids=[dst(d) for d in others], dma_engine_mask=eng(others[0], N - 1), remote_sem=M.amsg,
                                          srcs=[T.land3[r]], dsts=[T.land3[r] for d in others])], local_sem=M.xmsg)

    V(tc, T.lkf[:], T.lk[:])
    g.vector.wait_ge(M.gc3, 6)
    V(tc, T.e16[:], T.il16[:], dep=False)
    V(ts, T.edg[:], T.idg[:], T.q16f[:], None, A.add, dep=False)
    V(ms, T.zt[:], 0.0, dep=False)
    V(tc, T.kx[:], T.lkf[:].indirect(T.e16[:]))
    V(g.vector.quantize_mx, T.zq[:], T.zqs[:], T.zt[:], dep=False)
    V(tp, T.kg[:], T.kx[:])
    nz = n["v"]
    V(tc, T.kl[:, 0:256], T.kg[:].indirect(T.edg[:, 0:16]))
    V(tc, T.kl[:, 272:528], T.kg[:].indirect(T.edg[:, 16:32]), dep=False)
    V(ms, T.kl[:, 256:272], 70000.0, dep=False)
    V(ms, T.kl[:, 528:544], 70000.0, dep=False)
    V(ms, T.L[:, 0:576], 0.0, dep=False)
    V(ms, T.yfin[:, ZC:ZE], 0.0, dep=False)
    V(ms, T.kf[:, ZC:ZE], -1.0, dep=False)
    V(ms, T.rk[:, ZC:ZE], -1.0, dep=False)
    V(ms, T.cmp2[:, FIN:FIN + 1], -256.0, dep=False)
    V(ms, T.cmp2[:, FIN + 1:FIN + 2], 257.0 - FIN, dep=False)
    V(ts, T.trash[:], T.itr[:], T.q16f[:], None, A.add, dep=False)
    V(ts, T.c1[:], T.blk[:], 2.0, 16.0, A.is_ge, A.mult, dep=False)
    V(ts, T.c4[:], T.halff[:], 16.0, -float(ZC), A.mult, A.add, dep=False)
    V(tt, T.c3[:], T.b96[:], T.c1[:], A.add)
    V(tt, T.c5[:], T.c3[:], T.c4[:], A.add)
    V(ts, T.vals2[:], T.iv[:], T.c5[:], None, A.add)
    g.vector.wait_ge(M.lw, 16)
    V(g.vector.quantize_mx, T.wq[:], T.wqs[:], T.wt[:], dep=False)
    nwq = n["v"]
    g.sync.wait_ge(M.v, nslot)
    g.sync.dma_start(T.fin[:, at(r):at(r) + CAPP].bitcast(dt.uint8), T.slot[:, CAPP * r:CAPP * r + CAPP].bitcast(dt.uint8)).then_inc(M.lfin, 16)
    g.sync.wait_ge(M.s, nslots)
    g.sync.dma_start(T.fins[:, at(r):at(r) + CAPP], T.slots[:, CAPP * r:CAPP * r + CAPP]).then_inc(M.lfin, 16)
    g.sync.wait_ge(M.v, nz)
    g.sync.dma_start(T.fin[:, ZC:ZE].bitcast(dt.uint8), T.zq[:, 0:16].bitcast(dt.uint8)).then_inc(M.lzero, 16)
    g.sync.dma_start(T.fins[:, ZC:ZE], T.zqs[:, 0:16]).then_inc(M.lzero, 16)
    g.sync.wait_ge(M.lmsg, 64)
    g.sync.wait_ge(M.amsg, N - 1)
    for h in range(2):
        g.sync.dma_start(T.ix[:, 4 * h:4 * h + 3], T.land3[h:N:2, r // 2:128:4, 3 * (r % 2):3 * (r % 2) + 3]).then_inc(M.lix, 16)

    g.vector.wait_ge(M.lix, 32)
    V(tc, T.k96[:, 0:48], T.kl[:, 0:272].indirect(T.ix[:, 0:3]))
    V(tc, T.k96[:, 48:96], T.kl[:, 272:544].indirect(T.ix[:, 4:7]), dep=False)
    nk = n["v"]
    g.scalar.wait_ge(M.v, nk)
    for x in range(4):
        o = x + 1 - 2 * (x % 2)
        act(T.kf[32 * x:32 * x + 32, at(2 * o):at(2 * o) + 96], T.k96[32 * o:32 * o + 32, :], AF.Copy, dep=not x)
    for x in range(4):
        V(tc, T.kf[32 * x:32 * x + 32, at(2 * x):at(2 * x) + 96], T.k96[32 * x:32 * x + 32, :], dep=not x)
    V(tp, T.kt[:], T.k96[:], dep=False)
    nkt = n["v"]
    ns = n["s"]
    g.vector.wait_ge(M.s, ns)
    V(tc, T.kf[64:128, 0:ZC], T.kf[0:64, 0:ZC])
    nkf = n["v"]
    g.scalar.wait_ge(M.v, nkt)
    act(T.kf[0:64, ZE:FIN], T.kf[64:128, ZE:FIN], AF.Copy)
    g.scalar.wait_ge(M.v, nkf)
    for k in range(2):
        act(T.junk2[:, FIN * k:FIN * k + FIN], T.kf[:], AF.Sign, dep=not k, bias=T.kt[:, 32 * k:32 * k + 1], scale=-1.0, accum_out=T.s2[:, k:k + 1])
    ns2 = n["s"]
    g.vector.wait_ge(M.s, ns + 1)
    V(ts, T.cmp2[:, 0:FIN], T.kf[:], T.kt[:, 64:65], 2.0, A.is_lt, A.mult)
    V(red, T.s2[:, 2:3], T.cmp2[:], AxisListType.X, A.add)
    hi = T.spf[:, r:r + 1] if r < N - 1 else 65536.0
    V(ts, T.inv[:], T.kt[:, 0:96:32], hi, None, A.is_ge, dep=False)
    V(tt, T.tr[:], T.inv[:], T.trash[:], A.mult)
    g.vector.wait_ge(M.s, ns2)
    V(ts, T.hi[:], T.s2[:], 1 / 32, (FIN - 48) / 32, A.mult, A.add)
    V(ts, T.pos[:], T.s2[:], 0.5, (FIN - 33) / 2, A.mult, A.add, dep=False)
    V(ts, T.h16[:], T.hi[:], 16.0, None, A.mult)
    V(ts, T.h32[:], T.hi[:], 16.0, 16.0, A.mult, A.add, dep=False)
    for k in range(6):
        c = k % 3
        V(ts, T.ou[:, k:k + 1], T.pos[:, c:c + 1], T.tr[:, c:c + 1], (T.h32 if k > 2 else T.h16)[:, c:c + 1], A.max, A.add, dep=not k)
    V(tc, T.L[:].indirect(T.ou[:]), T.vals2[:])
    V(tp, T.LT[:], T.L[:, 0:576])
    V(tt, T.g1[:], T.LT[0:64, 0:576:16], T.LT[64:128, 0:576:16], A.add)
    V(tt, T.g2[:], T.g1[0:32, :], T.g1[32:64, :], A.add)
    V(tt, T.g3[:], T.g2[:, 0:36:2], T.g2[:, 1:36:2], A.add)
    for a in range(4):
        V(ts, T.ol[32 * a:32 * a + 32, :], T.g3[:], float(ZC), None, A.add, dep=not a)
    nol = n["v"]

    g.tensor.wait_ge(M.v, nwq)
    g.tensor.wait_ge(M.lfin, 32)
    g.tensor.wait_ge(M.acode, N - 1)
    g.tensor.wait_ge(M.ascale, N - 1)
    for i, a in enumerate((0, ZE)):
        if i:
            g.tensor.wait_ge(M.mm, 1)
        g.tensor.matmul_mx(T.acc[:, 512 * i:512 * i + ZC], T.wq[:], T.wqs[:], T.fin[:, a:a + ZC], T.fins[:, a:a + ZC], True, True).then_inc(M.mm, 1)
        g.scalar.wait_ge(M.mm, i + 1)
        act(T.yfin[:, a:a + ZC], T.acc[:, 512 * i:512 * i + ZC], AF.Copy)
    ny = n["s"]
    g.vector.wait_ge(M.lzero, 32)
    g.vector.wait_ge(M.lfin, 32)
    g.vector.wait_ge(M.acode, N - 1)
    V(tc, T.ord[:].bitcast(dt.uint32), T.fin[:].bitcast(dt.uint32).indirect(T.ol[:]))
    g.sync.wait_ge(M.v, n["v"])
    g.sync.dma_start(T.oc[:], T.ord[:].bitcast(dt.uint8)).then_inc(M.st, 16)
    g.vector.wait_ge(M.s, ny)
    V(tc, T.ysb[:], T.yfin[:].indirect(T.ol[:]))
    g.scalar.wait_ge(M.v, nol)
    g.scalar.wait_ge(M.lzero, 32)
    g.scalar.wait_ge(M.lfin, 32)
    g.scalar.wait_ge(M.ascale, N - 1)
    act(T.ords[:], T.fins[:].indirect(T.ol[:]), AF.Copy)
    g.sync.wait_ge(M.s, n["s"])
    for k in range(4):
        g.sync.dma_start(T.osc[4 * k:4 * k + 4, :], T.ords[32 * k:32 * k + 4, :]).then_inc(M.st, 16)
    g.sync.wait_ge(M.v, n["v"])
    g.sync.dma_start(T.y[:], T.ysb[:]).then_inc(M.st, 16)
    for i, (a, b) in enumerate(((T.kf, T.okk), (T.rk, T.okr))):
        act(b[:], a[:].indirect(T.ol[:]), AF.Copy)
        g.sync.wait_ge(M.s, n["s"])
        g.sync.dma_start(T.ok[i:i + 1, :], b[0:1, :]).then_inc(M.st, 16)
    g.wait_ge(M.xkey, N - 1)
    g.wait_ge(M.xcode, N - 1)
    g.wait_ge(M.xscale, N - 1)
    g.wait_ge(M.xmsg, 1)
    g.sync.wait_ge(M.st, 16 * 8)
